import numpy as np
import ml_dtypes


def mxq(x, axis, fmt="e4m3"):
    dtype, down = {"e4m3": (ml_dtypes.float8_e4m3fn, 7), "e5m2": (ml_dtypes.float8_e5m2, 14)}[fmt]
    v = np.moveaxis(np.asarray(x, np.float32).astype(ml_dtypes.bfloat16).astype(np.float64), axis, -1)
    blocks = v.reshape(v.shape[:-1] + (-1, 32))
    amax = np.abs(blocks).max(-1, keepdims=True)
    byte = np.maximum(np.where(amax > 0, np.frexp(amax)[1] - 1 + 127, 0) - down, 1)
    scale = np.exp2(byte - 127.0)
    codes = (blocks / scale).astype(np.float32).astype(dtype).astype(np.float64)
    return np.moveaxis((codes * scale).reshape(v.shape), -1, axis)


WIDE = False


def mx_kscale(k):
    if not WIDE:
        return np.ones(k)
    levels = np.array([10, -10, 5, -5, 0])
    if k % 512:
        return np.exp2(np.random.permutation(np.resize(levels, k // 32))).repeat(32)
    a = np.empty((k // 512, 16))
    for p in range(k // 512):
        a[p, :8] = np.random.permutation(np.resize(levels, 8))
        for g in range(8):
            far = levels[np.abs(levels - a[p, g]) >= 10]
            a[p, g + 8] = far[np.random.randint(len(far))]
    return np.exp2(a.ravel()).repeat(32)


def f64(x):
    return np.asarray(x).astype(np.float64)


def striped(idx):
    return np.tile(idx.reshape(-1, 16).T, (8, 1)).astype(np.uint16)


def unstriped(offs):
    return offs[:16].T.reshape(-1).astype(np.int64)


def striped8(idx):
    return np.concatenate([x.reshape(-1, 16).T for x in idx]).astype(np.uint16)


def runs(offs, k):
    lists = np.stack([offs[16 * r : 16 * r + 16].T.reshape(-1) for r in range(8)]).astype(np.int64)
    return lists[np.arange(k) % 512 // 64]


def pack_weight(w):
    k, n = w.shape
    w = f64(np.asarray(w, np.float32).astype(ml_dtypes.bfloat16)).reshape(k // 32, 32, n)
    amax = np.abs(w).max(1)
    byte = np.clip(np.where(amax > 0, np.frexp(amax)[1] - 1 + 127 - 7, 1), 1, 254)
    scaled = (w * np.exp2(127.0 - byte)[:, None, :]).reshape(k, n).astype(np.float32)
    words = np.ascontiguousarray(scaled.reshape(k // 512, 128, 4, n).transpose(0, 1, 3, 2)).astype(ml_dtypes.float8_e4m3fn).view(np.uint8)
    return words, np.ascontiguousarray(byte.astype(np.uint8).reshape(k // 512, 16, n))


def unpack_weight(words, scales):
    g, p, n, _ = words.shape
    vals = np.ascontiguousarray(words).view(ml_dtypes.float8_e4m3fn).astype(np.float64) * np.repeat(np.exp2(scales.astype(np.float64) - 127.0), 8, axis=1)[..., None]
    return vals.transpose(0, 1, 3, 2).reshape(g * 512, n)


def relu(v):
    return np.maximum(v, 0.0)


K, T, S, N, H = 512, 2048, 512, 512, 512


def setup_inputs():
    n = np.random.standard_normal
    s = mx_kscale(K)[:, None]
    u = mx_kscale(H)
    packed_xT = pack_weight(n((K, T)) * s)
    return {
        "x_words": packed_xT[0],
        "x_scales": packed_xT[1],
        "w1": (n((K, H)) / np.sqrt(K) / s).astype(np.float32),
        "w2": (n((K, H)) / np.sqrt(K) / s).astype(np.float32),
        "gn": (np.random.uniform(0.5, 1.5, (H, 1)) * u[:, None]).astype(np.float32),
        "w3": (n((H, N)) / np.sqrt(H) / u[:, None]).astype(np.float32),
        "offs": striped(np.random.permutation(T)[:S]),
        "two": striped(np.random.permutation(T)[:S]),
        "n1": striped8(np.stack([np.random.permutation(S) for _ in range(8)])),
        "n2": striped8(np.stack([np.random.permutation(S) for _ in range(8)])),
        "n3": striped8(np.stack([np.random.permutation(S) for _ in range(8)])),
        "n4": striped8(np.stack([np.random.permutation(S) for _ in range(8)])),
        "n5": striped8(np.stack([np.random.permutation(S) for _ in range(8)])),
    }


def reference(x_words, x_scales, w1, w2, gn, w3, offs, two, n1, n2, n3, n4, n5):
    xq = unpack_weight(x_words, x_scales)[:, unstriped(offs)]
    y = mxq(f64(w1), 0, "e4m3").T @ xq
    x_two = unpack_weight(x_words, x_scales)[:, unstriped(two)]
    d = mxq(f64(w2), 0, "e4m3").T @ x_two
    z = f64(gn) * (np.maximum(np.minimum(y - (0.5 * (y[np.arange(H)[:, None], runs(n1, H)])), d[np.arange(H)[:, None], runs(n2, H)]), d[np.arange(H)[:, None], runs(n3, H)]))
    h = mxq(f64(w3), 0, "e4m3").T @ mxq(z, 0, "e4m3")
    pa = h - (h[np.arange(N)[:, None], runs(n4, N)])
    pb = h[np.arange(N)[:, None], runs(n5, N)] - h
    return relu(np.minimum(pa, pb)) - (relu(-1.0 * np.maximum(pa, pb)))

@@ -1,0 +1,228 @@
+from contextlib import ExitStack
+
+import concourse.mybir as mybir
+
+K, T, S, N, H = 512, 2048, 512, 512, 512
+FLOPS = 2 * S * (2 * K * H + H * N)
+
+F32 = mybir.dt.float32
+BF16 = mybir.dt.bfloat16
+I32 = mybir.dt.int32
+U32 = mybir.dt.uint32
+U16 = mybir.dt.uint16
+U8 = mybir.dt.uint8
+FP8X4 = mybir.dt.float8_e4m3fn_x4
+ALU = mybir.AluOpType
+ACT = mybir.ActivationFunctionType
+
+P = 128
+PACK = 4
+HALF = S // 2
+LCOLS = HALF // 16
+
+
+def tile_picked_twlclampbminmod_none_p_kernel(
+    tc, x_words, x_scales, w1, w2, gn, w3, offs, two, n1, n2, n3, n4, n5, out
+):
+    nc = tc.nc
+    with ExitStack() as ctx:
+        lists = ctx.enter_context(tc.tile_pool(name="lists", bufs=1))
+        sb = ctx.enter_context(tc.tile_pool(name="sb", bufs=1))
+        psum = ctx.enter_context(tc.psum_pool(name="psum", bufs=1))
+
+        def load_list(name, src):
+            dst = lists.tile([P, S // 16], U16, name=name)
+            nc.sync.dma_start(dst[:], src)
+            return dst
+
+        def load_weight(name, src):
+            dst = sb.tile([P, PACK, 512], F32, name=name)
+            nc.sync.dma_start(dst[:], src.rearrange("(p j) c -> p j c", j=PACK))
+            return dst
+
+        table_scales = sb.tile([P, T], U8, name="table_scales", align_bytes=64)
+        nc.vector.memset(table_scales[:].bitcast(I32), 0)
+
+        gain = sb.tile([P, PACK], F32, name="gain")
+        nc.sync.dma_start(gain[:], gn.rearrange("(p t) o -> p (t o)", t=PACK))
+        two_sb = load_list("two_sb", two)
+        for q in range(4):
+            nc.scalar.dma_start(
+                table_scales[32 * q : 32 * q + 4, :].bitcast(I32), x_scales[0, 4 * q : 4 * q + 4, :].bitcast(I32)
+            )
+        table_words = sb.tile([P, T], I32, name="table_words", align_bytes=64)
+        nc.sync.dma_start(table_words[:], x_words[0].rearrange("p n r -> p (n r)").bitcast(I32))
+        offs_sb = load_list("offs_sb", offs)
+        w2_raw = load_weight("w2_raw", w2)
+        n2_sb = load_list("n2_sb", n2)
+        w1_raw = load_weight("w1_raw", w1)
+        n3_sb = load_list("n3_sb", n3)
+        n1_sb = load_list("n1_sb", n1)
+        w3_raw = load_weight("w3_raw", w3)
+        n4_sb = load_list("n4_sb", n4)
+        n5_sb = load_list("n5_sb", n5)
+
+        gain_abs = sb.tile([P, PACK], F32, name="gain_abs")
+        nc.scalar.activation(gain_abs[:], gain[:], ACT.Abs)
+        gain_half = sb.tile([P, PACK], F32, name="gain_half")
+        nc.scalar.activation(gain_half[:], gain_abs[:], ACT.Copy, scale=-0.5)
+        gain_ge = sb.tile([P, PACK], F32, name="gain_ge")
+        nc.gpsimd.tensor_scalar(gain_ge[:], gain[:], 0.0, 2.0, ALU.is_ge, ALU.mult)
+        gain_sign = sb.tile([P, PACK], F32, name="gain_sign")
+        nc.gpsimd.tensor_scalar(gain_sign[:], gain_ge[:], 1.0, -1.0, ALU.mult, ALU.add)
+
+        def pick(name, window, offsets, dtype, tag=""):
+            dst = sb.tile([P, S], dtype, name=name, tag=tag, align_bytes=64)
+            nc.vector.tensor_copy(dst[:], window.indirect(offsets[:]))
+            return dst
+
+        def deal(dealt, raw, pair, copy):
+            copy(
+                dealt.rearrange("p t m j -> p m j t"),
+                raw[:].rearrange("p j (m t) -> p m j t", t=PACK)[:, :, :, 2 * pair : 2 * pair + 2],
+            )
+
+        def pair_tile(name):
+            return sb.tile([P, 2, P, PACK], BF16, name=name, align_bytes=64)
+
+        def quantize(name, values, width):
+            codes = sb.tile([P, width], U32, name=name + "_codes", align_bytes=64)
+            scales = sb.tile([P, width], U8, name=name + "_scales", align_bytes=64)
+            nc.vector.quantize_mx(codes[:].bitcast(FP8X4), scales[:], values)
+            return codes, scales
+
+        def quantize_weight(name, dealt):
+            return quantize(name, dealt.rearrange("p t m j -> p (t m j)"), 2 * P)
+
+        def product(dst, weight, t, codes, scales):
+            w_codes, w_scales = weight[t // 2]
+            cols = slice((t % 2) * P, (t % 2 + 1) * P)
+            nc.tensor.matmul_mx(
+                dst, lhsT=w_codes[:, cols].bitcast(FP8X4), lhsT_scale=w_scales[:, cols],
+                rhs=codes[:].bitcast(FP8X4), rhs_scale=scales[:], start=True, stop=True,
+            )
+
+        def half(c):
+            return slice(c * HALF, (c + 1) * HALF)
+
+        def look(window, offsets, c):
+            return window[:].indirect(offsets[:, c * LCOLS : (c + 1) * LCOLS])
+
+        banks = [psum.tile([P, S], F32, name="bank%d" % b) for b in range(8)]
+
+        x2_words = pick("x2_words", table_words[:].bitcast(U32), two_sb, U32)
+        x2_scales = pick("x2_scales", table_scales[:], two_sb, U8)
+        x1_words = pick("x1_words", table_words[:].bitcast(U32), offs_sb, U32)
+        w2_a, w2_b = pair_tile("w2_a"), pair_tile("w2_b")
+        deal(w2_a[:], w2_raw, 0, nc.scalar.copy)
+        deal(w2_b[:], w2_raw, 1, nc.scalar.copy)
+        w2_q = [quantize_weight("w2_qa", w2_a[:])]
+        x1_scales = pick("x1_scales", table_scales[:], offs_sb, U8, tag="w2_a")
+        w2_q.append(quantize_weight("w2_qb", w2_b[:]))
+
+        d = []
+        for t in range(PACK):
+            product(banks[PACK + t][:], w2_q, t, x2_words, x2_scales)
+            d.append(sb.tile([P, S], F32, name="d%d" % t))
+            nc.scalar.activation(d[t][:], banks[PACK + t][:], ACT.Copy, scale=gain_abs[:, t : t + 1])
+
+        w1_dealt = sb.tile([P, PACK, P, PACK], BF16, name="w1_dealt", tag="w1_then_d3", align_bytes=64)
+        for pair in range(2):
+            deal(w1_dealt[:, 2 * pair : 2 * pair + 2], w1_raw, pair, nc.scalar.copy)
+
+        a = [sb.tile([P, PACK, HALF], F32, name="a%d" % c) for c in range(2)]
+        d2 = [sb.tile([P, PACK, HALF], F32, name="d2_%d" % c) for c in range(2)]
+
+        def gather_d(dst, offsets, c, t):
+            nc.vector.tensor_copy(dst[:, t, :], look(d[t], offsets, c))
+
+        for t in range(PACK):
+            for c in range(2):
+                gather_d(d2[c], n2_sb, c, t)
+        w1_q = [quantize_weight("w1_q%d" % pair, w1_dealt[:, 2 * pair : 2 * pair + 2]) for pair in range(2)]
+        d3_first = sb.tile([P, PACK, HALF], F32, name="d3_first", tag="w1_then_d3", align_bytes=64)
+        d3 = [d3_first, d2[0]]
+        for t in range(PACK):
+            gather_d(d3[0], n3_sb, 0, t)
+
+        y, y_half = [], []
+        for t in range(PACK):
+            product(banks[t][:], w1_q, t, x1_words, x1_scales)
+            y.append(sb.tile([P, S], F32, name="y%d" % t))
+            y_half.append(sb.tile([P, S], F32, name="y_half%d" % t))
+            nc.scalar.activation(y_half[t][:], banks[t][:], ACT.Copy, scale=gain_half[:, t : t + 1])
+            nc.scalar.activation(y[t][:], banks[t][:], ACT.Copy, scale=gain_abs[:, t : t + 1])
+            for c in range(2):
+                nc.vector.tensor_tensor(a[c][:, t, :], look(y_half[t], n1_sb, c), y[t][:, half(c)], ALU.add)
+
+        for j in range(PACK):
+            nc.scalar.activation(w3_raw[:, j, :], w3_raw[:, j, :], ACT.Copy, scale=gain_sign[:, j : j + 1])
+        w3_a, w3_b = pair_tile("w3_a"), pair_tile("w3_b")
+        deal(w3_a[:], w3_raw, 0, nc.scalar.copy)
+        deal(w3_b[:], w3_raw, 1, nc.scalar.copy)
+
+        h = [sb.tile([P, S], F32, name="h%d" % t) for t in range(PACK)]
+        h_neg = [sb.tile([P, S], F32, name="h_neg%d" % t) for t in range(PACK)]
+        z = [sb.tile([P, HALF, PACK], BF16, name="z%d" % c, align_bytes=64) for c in range(2)]
+
+        def smaller(c):
+            nc.vector.tensor_tensor(a[c][:], a[c][:], d2[c][:], ALU.min)
+
+        def larger(c):
+            runs = "p t (g i) -> p g t i"
+            nc.vector.tensor_tensor(
+                z[c][:].rearrange("p (g i) t -> p g t i", i=4),
+                a[c][:].rearrange(runs, i=4), d3[c][:].rearrange(runs, i=4), ALU.max,
+            )
+
+        def second_layer(c, z_q):
+            for t in range(PACK):
+                bank = banks[PACK * (1 - c) + t]
+                product(bank[:, 0:HALF], w3_q, t, z_q[0], z_q[1])
+                nc.scalar.activation(h_neg[t][:, half(c)], bank[:, 0:HALF], ACT.Copy, scale=-1.0)
+                nc.scalar.copy(h[t][:, half(c)], bank[:, 0:HALF])
+
+        smaller(0)
+        smaller(1)
+        larger(0)
+        w3_q = [quantize_weight("w3_qa", w3_a[:]), quantize_weight("w3_qb", w3_b[:])]
+        second_layer(0, quantize("z0", z[0][:].rearrange("p s t -> p (s t)"), HALF))
+        for t in range(PACK):
+            gather_d(d3[1], n3_sb, 1, t)
+        larger(1)
+        second_layer(1, quantize("z1", z[1][:].rearrange("p s t -> p (s t)"), HALF))
+
+        pa = [sb.tile([P, S], F32, name="pa%d" % t) for t in range(PACK)]
+        pb = [sb.tile([P, S], F32, name="pb%d" % t) for t in range(PACK)]
+        res = [sb.tile([P, S], F32, name="res%d" % t) for t in range(PACK)]
+        out_rows = out.rearrange("(p t) s -> t p s", t=PACK)
+
+        def gather_pa(t, c):
+            nc.vector.tensor_tensor(pa[t][:, half(c)], look(h_neg[t], n4_sb, c), h[t][:, half(c)], ALU.add)
+
+        def gather_pb(t, c):
+            nc.vector.tensor_tensor(pb[t][:, half(c)], look(h[t], n5_sb, c), h_neg[t][:, half(c)], ALU.add)
+
+        def lower(t, cols):
+            nc.vector.scalar_tensor_tensor(pa[t][:, cols], pb[t][:, cols], 0.0, pa[t][:, cols], ALU.min, ALU.max)
+
+        def upper(t, cols):
+            nc.vector.scalar_tensor_tensor(res[t][:, cols], pb[t][:, cols], 0.0, pa[t][:, cols], ALU.max, ALU.min)
+            nc.sync.dma_start(out_rows[t][:, cols], res[t][:, cols])
+
+        every = slice(0, S)
+        last = PACK - 1
+        for t in range(PACK):
+            gather_pa(t, 0)
+            if t > 0:
+                lower(t - 1, every)
+            gather_pb(t, 0)
+            if t > 0:
+                upper(t - 1, every)
+            gather_pa(t, 1)
+            if t == last:
+                lower(t, half(0))
+            gather_pb(t, 1)
+        upper(last, half(0))
+        lower(last, half(1))
+        upper(last, half(1))

@@ -18,7 +18,7 @@ ACT = mybir.ActivationFunctionType
 P = 128
 PACK = 4
 HALF = S // 2
-LCOLS = HALF // 16
+RUN = 8
 
 
 def tile_picked_twlclampbminmod_none_p_kernel(
@@ -43,17 +43,17 @@ def tile_picked_twlclampbminmod_none_p_kernel(
         table_scales = sb.tile([P, T], U8, name="table_scales", align_bytes=64)
         nc.vector.memset(table_scales[:].bitcast(I32), 0)
 
-        gain = sb.tile([P, PACK], F32, name="gain")
-        nc.sync.dma_start(gain[:], gn.rearrange("(p t) o -> p (t o)", t=PACK))
-        two_sb = load_list("two_sb", two)
         for q in range(4):
             nc.scalar.dma_start(
                 table_scales[32 * q : 32 * q + 4, :].bitcast(I32), x_scales[0, 4 * q : 4 * q + 4, :].bitcast(I32)
             )
         table_words = sb.tile([P, T], I32, name="table_words", align_bytes=64)
         nc.sync.dma_start(table_words[:], x_words[0].rearrange("p n r -> p (n r)").bitcast(I32))
+        two_sb = load_list("two_sb", two)
         offs_sb = load_list("offs_sb", offs)
         w2_raw = load_weight("w2_raw", w2)
+        gain = sb.tile([P, PACK], F32, name="gain")
+        nc.sync.dma_start(gain[:], gn.rearrange("(p t) o -> p (t o)", t=PACK))
         n2_sb = load_list("n2_sb", n2)
         w1_raw = load_weight("w1_raw", w1)
         n3_sb = load_list("n3_sb", n3)
@@ -62,14 +62,11 @@ def tile_picked_twlclampbminmod_none_p_kernel(
         n4_sb = load_list("n4_sb", n4)
         n5_sb = load_list("n5_sb", n5)
 
-        gain_abs = sb.tile([P, PACK], F32, name="gain_abs")
-        nc.scalar.activation(gain_abs[:], gain[:], ACT.Abs)
-        gain_half = sb.tile([P, PACK], F32, name="gain_half")
-        nc.scalar.activation(gain_half[:], gain_abs[:], ACT.Copy, scale=-0.5)
-        gain_ge = sb.tile([P, PACK], F32, name="gain_ge")
-        nc.gpsimd.tensor_scalar(gain_ge[:], gain[:], 0.0, 2.0, ALU.is_ge, ALU.mult)
-        gain_sign = sb.tile([P, PACK], F32, name="gain_sign")
-        nc.gpsimd.tensor_scalar(gain_sign[:], gain_ge[:], 1.0, -1.0, ALU.mult, ALU.add)
+        wide_a = [sb.tile([P, 2 * S], F32, name="wide_a%d" % t) for t in range(PACK)]
+        wide_b = [sb.tile([P, 2 * S], F32, name="wide_b%d" % t) for t in range(PACK)]
+        d = [sb.tile([P, 2 * S], F32, name="d%d" % t) for t in range(PACK)]
+        for wide in d + wide_a[:1]:
+            nc.vector.memset(wide[:, S:], 0.0)
 
         def pick(name, window, offsets, dtype, tag=""):
             dst = sb.tile([P, S], dtype, name=name, tag=tag, align_bytes=64)
@@ -85,123 +82,153 @@ def tile_picked_twlclampbminmod_none_p_kernel(
         def pair_tile(name):
             return sb.tile([P, 2, P, PACK], BF16, name=name, align_bytes=64)
 
-        def quantize(name, values, width):
-            codes = sb.tile([P, width], U32, name=name + "_codes", align_bytes=64)
+        def quantize(name, values, width, tag=""):
+            codes = sb.tile([P, width], U32, name=name + "_codes", tag=tag, align_bytes=64)
             scales = sb.tile([P, width], U8, name=name + "_scales", align_bytes=64)
             nc.vector.quantize_mx(codes[:].bitcast(FP8X4), scales[:], values)
             return codes, scales
 
-        def quantize_weight(name, dealt):
-            return quantize(name, dealt.rearrange("p t m j -> p (t m j)"), 2 * P)
+        def quantize_weight(name, dealt, tag=""):
+            return column_tiles(quantize(name, dealt.rearrange("p t m j -> p (t m j)"), dealt.shape[1] * P, tag))
 
-        def product(dst, weight, t, codes, scales):
-            w_codes, w_scales = weight[t // 2]
-            cols = slice((t % 2) * P, (t % 2 + 1) * P)
+        def product(dst, weight, codes, scales):
             nc.tensor.matmul_mx(
-                dst, lhsT=w_codes[:, cols].bitcast(FP8X4), lhsT_scale=w_scales[:, cols],
-                rhs=codes[:].bitcast(FP8X4), rhs_scale=scales[:], start=True, stop=True,
+                dst, lhsT=weight[0].bitcast(FP8X4), lhsT_scale=weight[1],
+                rhs=codes.bitcast(FP8X4), rhs_scale=scales, start=True, stop=True,
             )
+
+        def column_tiles(quantized):
+            codes, scales = quantized
+            return [(codes[:, c : c + P], scales[:, c : c + P]) for c in range(0, codes.shape[1], P)]
 
         def half(c):
             return slice(c * HALF, (c + 1) * HALF)
 
-        def look(window, offsets, c):
-            return window[:].indirect(offsets[:, c * LCOLS : (c + 1) * LCOLS])
+        def look(window, offsets, cols):
+            return window[:].indirect(offsets[:, cols.start // 16 : cols.stop // 16])
 
         banks = [psum.tile([P, S], F32, name="bank%d" % b) for b in range(8)]
 
         x2_words = pick("x2_words", table_words[:].bitcast(U32), two_sb, U32)
-        x2_scales = pick("x2_scales", table_scales[:], two_sb, U8)
         x1_words = pick("x1_words", table_words[:].bitcast(U32), offs_sb, U32)
+        x2_scales = pick("x2_scales", table_scales[:], two_sb, U8)
         w2_a, w2_b = pair_tile("w2_a"), pair_tile("w2_b")
         deal(w2_a[:], w2_raw, 0, nc.scalar.copy)
-        deal(w2_b[:], w2_raw, 1, nc.scalar.copy)
-        w2_q = [quantize_weight("w2_qa", w2_a[:])]
+        deal(w2_b[:], w2_raw, 1, nc.vector.tensor_copy)
+        w2_q = quantize_weight("w2_qa", w2_a[:]) + quantize_weight("w2_qb", w2_b[:])
         x1_scales = pick("x1_scales", table_scales[:], offs_sb, U8, tag="w2_a")
-        w2_q.append(quantize_weight("w2_qb", w2_b[:]))
 
-        d = []
+        gain_abs = sb.tile([P, PACK], F32, name="gain_abs")
+        nc.scalar.activation(gain_abs[:], gain[:], ACT.Abs)
+        gain_half = sb.tile([P, PACK], F32, name="gain_half")
+        nc.scalar.activation(gain_half[:], gain_abs[:], ACT.Copy, scale=-0.5)
+        gain_ge = sb.tile([P, PACK], F32, name="gain_ge")
+        nc.gpsimd.tensor_scalar(gain_ge[:], gain[:], 0.0, 2.0, ALU.is_ge, ALU.mult)
+        gain_sign = sb.tile([P, PACK], F32, name="gain_sign")
+        nc.gpsimd.tensor_scalar(gain_sign[:], gain_ge[:], 1.0, -1.0, ALU.mult, ALU.add)
+
         for t in range(PACK):
-            product(banks[PACK + t][:], w2_q, t, x2_words, x2_scales)
-            d.append(sb.tile([P, S], F32, name="d%d" % t))
-            nc.scalar.activation(d[t][:], banks[PACK + t][:], ACT.Copy, scale=gain_abs[:, t : t + 1])
+            product(banks[PACK + t][:], w2_q[t], x2_words[:], x2_scales[:])
+            nc.scalar.activation(d[t][:, 0:S], banks[PACK + t][:], ACT.Copy, scale=gain_abs[:, t : t + 1])
 
         w1_dealt = sb.tile([P, PACK, P, PACK], BF16, name="w1_dealt", tag="w1_then_d3", align_bytes=64)
         for pair in range(2):
             deal(w1_dealt[:, 2 * pair : 2 * pair + 2], w1_raw, pair, nc.scalar.copy)
 
-        a = [sb.tile([P, PACK, HALF], F32, name="a%d" % c) for c in range(2)]
-        d2 = [sb.tile([P, PACK, HALF], F32, name="d2_%d" % c) for c in range(2)]
-
-        def gather_d(dst, offsets, c, t):
-            nc.vector.tensor_copy(dst[:, t, :], look(d[t], offsets, c))
-
+        every = slice(0, S)
+        d2 = sb.tile([P, PACK, S], BF16, name="d_n2", align_bytes=64)
         for t in range(PACK):
-            for c in range(2):
-                gather_d(d2[c], n2_sb, c, t)
-        w1_q = [quantize_weight("w1_q%d" % pair, w1_dealt[:, 2 * pair : 2 * pair + 2]) for pair in range(2)]
-        d3_first = sb.tile([P, PACK, HALF], F32, name="d3_first", tag="w1_then_d3", align_bytes=64)
-        d3 = [d3_first, d2[0]]
-        for t in range(PACK):
-            gather_d(d3[0], n3_sb, 0, t)
+            nc.vector.tensor_copy(d2[:, t, :], look(d[t], n2_sb, every))
+        w1_q = quantize_weight("w1_qa", w1_dealt[:, 0:2]) + quantize_weight("w1_qb", w1_dealt[:, 2:4])
 
-        y, y_half = [], []
-        for t in range(PACK):
-            product(banks[t][:], w1_q, t, x1_words, x1_scales)
-            y.append(sb.tile([P, S], F32, name="y%d" % t))
-            y_half.append(sb.tile([P, S], F32, name="y_half%d" % t))
-            nc.scalar.activation(y_half[t][:], banks[t][:], ACT.Copy, scale=gain_half[:, t : t + 1])
-            nc.scalar.activation(y[t][:], banks[t][:], ACT.Copy, scale=gain_abs[:, t : t + 1])
-            for c in range(2):
-                nc.vector.tensor_tensor(a[c][:, t, :], look(y_half[t], n1_sb, c), y[t][:, half(c)], ALU.add)
+        def gather_d3(c, t):
+            nc.vector.tensor_copy(d3[c][:, t, :], look(d[t], n3_sb, half(c)))
 
-        for j in range(PACK):
+        def sign_w3(j):
             nc.scalar.activation(w3_raw[:, j, :], w3_raw[:, j, :], ACT.Copy, scale=gain_sign[:, j : j + 1])
+
+        a_round = sb.tile([P, PACK, S], BF16, name="a_round")
+        d3_first = sb.tile([P, PACK, HALF], BF16, name="d3_first", tag="w1_then_d3", align_bytes=64)
+        d3 = [d3_first[:], a_round[:, :, half(0)]]
+        for t in range(PACK):
+            gather_d3(0, t)
+        sign_w3(0)
+        sign_w3(1)
+
+        y_half = wide_a
+        y_last = sb.tile([P, S], F32, name="y3", align_bytes=64)
+        y = [wide_a[t + 1][:, S:] for t in range(PACK - 1)] + [y_last[:]]
+        a = [wide_b[t][:, S:] for t in range(PACK)]
+        for t in range(PACK):
+            product(banks[t][:], w1_q[t], x1_words[:], x1_scales[:])
+            nc.scalar.activation(y_half[t][:, every], banks[t][:], ACT.Copy, scale=gain_half[:, t : t + 1])
+            nc.scalar.activation(y[t], banks[t][:], ACT.Copy, scale=gain_abs[:, t : t + 1])
+            nc.vector.tensor_tensor(a[t], look(y_half[t], n1_sb, every), y[t], ALU.add)
+        for t in range(PACK):
+            nc.scalar.copy(a_round[:, t, :], a[t])
+
+        sign_w3(2)
+        sign_w3(3)
         w3_a, w3_b = pair_tile("w3_a"), pair_tile("w3_b")
         deal(w3_a[:], w3_raw, 0, nc.scalar.copy)
         deal(w3_b[:], w3_raw, 1, nc.scalar.copy)
 
-        h = [sb.tile([P, S], F32, name="h%d" % t) for t in range(PACK)]
-        h_neg = [sb.tile([P, S], F32, name="h_neg%d" % t) for t in range(PACK)]
+        last = PACK - 1
         z = [sb.tile([P, HALF, PACK], BF16, name="z%d" % c, align_bytes=64) for c in range(2)]
+        z_codes = sb.tile([P, S], U32, name="z_codes", align_bytes=64)
+        z_scales = sb.tile([P, S], U8, name="z_scales", align_bytes=64)
 
-        def smaller(c):
-            nc.vector.tensor_tensor(a[c][:], a[c][:], d2[c][:], ALU.min)
+        def smaller(tiles):
+            nc.vector.tensor_tensor(d2[:, tiles, :], d2[:, tiles, :], a_round[:, tiles, :], ALU.min)
 
         def larger(c):
             runs = "p t (g i) -> p g t i"
             nc.vector.tensor_tensor(
-                z[c][:].rearrange("p (g i) t -> p g t i", i=4),
-                a[c][:].rearrange(runs, i=4), d3[c][:].rearrange(runs, i=4), ALU.max,
+                z[c][:].rearrange("p (g i) t -> p g t i", i=RUN),
+                d2[:, :, half(c)].rearrange(runs, i=RUN), d3[c].rearrange(runs, i=RUN), ALU.max,
             )
 
-        def second_layer(c, z_q):
-            for t in range(PACK):
-                bank = banks[PACK * (1 - c) + t]
-                product(bank[:, 0:HALF], w3_q, t, z_q[0], z_q[1])
-                nc.scalar.activation(h_neg[t][:, half(c)], bank[:, 0:HALF], ACT.Copy, scale=-1.0)
-                nc.scalar.copy(h[t][:, half(c)], bank[:, 0:HALF])
+        def quantize_z(c):
+            nc.vector.quantize_mx(
+                z_codes[:, half(c)].bitcast(FP8X4), z_scales[:, half(c)], z[c][:].rearrange("p s t -> p (s t)")
+            )
 
-        smaller(0)
-        smaller(1)
+        smaller(slice(0, last))
+        gather_d3(1, 0)
+        smaller(slice(last, PACK))
+        gather_d3(1, 1)
         larger(0)
-        w3_q = [quantize_weight("w3_qa", w3_a[:]), quantize_weight("w3_qb", w3_b[:])]
-        second_layer(0, quantize("z0", z[0][:].rearrange("p s t -> p (s t)"), HALF))
-        for t in range(PACK):
-            gather_d(d3[1], n3_sb, 1, t)
+        w3_q = quantize_weight("w3_q0", w3_a[:, 0:1])
+        gather_d3(1, 2)
+        quantize_z(0)
+        gather_d3(1, 3)
         larger(1)
-        second_layer(1, quantize("z1", z[1][:].rearrange("p s t -> p (s t)"), HALF))
+        w3_q = w3_q + quantize_weight("w3_q1", w3_a[:, 1:2], tag="d_n2")
+        quantize_z(1)
+        w3_q = w3_q + quantize_weight("w3_qb", w3_b[:], tag="z1")
+
+        h, h_neg = wide_a, wide_b
+
+        def second_layer(t, cols, bank):
+            product(bank[:, cols], w3_q[t], z_codes[:, cols], z_scales[:, cols])
+            nc.scalar.activation(h_neg[t][:, cols], bank[:, cols], ACT.Copy, scale=-1.0)
+            nc.scalar.copy(h[t][:, cols], bank[:, cols])
+
+        second_layer(0, half(0), banks[PACK])
+        second_layer(0, half(1), banks[0])
+        for t in range(1, PACK):
+            second_layer(t, every, banks[t])
 
         pa = [sb.tile([P, S], F32, name="pa%d" % t) for t in range(PACK)]
         pb = [sb.tile([P, S], F32, name="pb%d" % t) for t in range(PACK)]
         res = [sb.tile([P, S], F32, name="res%d" % t) for t in range(PACK)]
         out_rows = out.rearrange("(p t) s -> t p s", t=PACK)
 
-        def gather_pa(t, c):
-            nc.vector.tensor_tensor(pa[t][:, half(c)], look(h_neg[t], n4_sb, c), h[t][:, half(c)], ALU.add)
+        def gather_pa(t, cols):
+            nc.vector.tensor_tensor(pa[t][:, cols], look(h_neg[t], n4_sb, cols), h[t][:, cols], ALU.add)
 
-        def gather_pb(t, c):
-            nc.vector.tensor_tensor(pb[t][:, half(c)], look(h[t], n5_sb, c), h_neg[t][:, half(c)], ALU.add)
+        def gather_pb(t, cols):
+            nc.vector.tensor_tensor(pb[t][:, cols], look(h[t], n5_sb, cols), h_neg[t][:, cols], ALU.add)
 
         def lower(t, cols):
             nc.vector.scalar_tensor_tensor(pa[t][:, cols], pb[t][:, cols], 0.0, pa[t][:, cols], ALU.min, ALU.max)
@@ -210,19 +237,20 @@ def tile_picked_twlclampbminmod_none_p_kernel(
             nc.vector.scalar_tensor_tensor(res[t][:, cols], pb[t][:, cols], 0.0, pa[t][:, cols], ALU.max, ALU.min)
             nc.sync.dma_start(out_rows[t][:, cols], res[t][:, cols])
 
-        every = slice(0, S)
-        last = PACK - 1
-        for t in range(PACK):
-            gather_pa(t, 0)
+        for t in range(last):
+            gather_pa(t, every)
             if t > 0:
                 lower(t - 1, every)
-            gather_pb(t, 0)
+            gather_pb(t, every)
             if t > 0:
                 upper(t - 1, every)
-            gather_pa(t, 1)
-            if t == last:
-                lower(t, half(0))
-            gather_pb(t, 1)
+        gather_pa(last, half(0))
+        lower(last - 1, every)
+        gather_pb(last, half(0))
+        upper(last - 1, every)
+        gather_pa(last, half(1))
+        lower(last, half(0))
+        gather_pb(last, half(1))
         upper(last, half(0))
         lower(last, half(1))
         upper(last, half(1))

@@ -43,14 +43,14 @@ def tile_picked_twlclampbminmod_none_p_kernel(
         table_scales = sb.tile([P, T], U8, name="table_scales", align_bytes=64)
         nc.vector.memset(table_scales[:].bitcast(I32), 0)
 
-        for q in range(4):
-            nc.scalar.dma_start(
-                table_scales[32 * q : 32 * q + 4, :].bitcast(I32), x_scales[0, 4 * q : 4 * q + 4, :].bitcast(I32)
-            )
         table_words = sb.tile([P, T], I32, name="table_words", align_bytes=64)
         nc.sync.dma_start(table_words[:], x_words[0].rearrange("p n r -> p (n r)").bitcast(I32))
         two_sb = load_list("two_sb", two)
         offs_sb = load_list("offs_sb", offs)
+        for q in range(4):
+            nc.sync.dma_start(
+                table_scales[32 * q : 32 * q + 4, :].bitcast(I32), x_scales[0, 4 * q : 4 * q + 4, :].bitcast(I32)
+            )
         w2_raw = load_weight("w2_raw", w2)
         gain = sb.tile([P, PACK], F32, name="gain")
         nc.sync.dma_start(gain[:], gn.rearrange("(p t) o -> p (t o)", t=PACK))
@@ -114,9 +114,10 @@ def tile_picked_twlclampbminmod_none_p_kernel(
         x2_scales = pick("x2_scales", table_scales[:], two_sb, U8)
         w2_a, w2_b = pair_tile("w2_a"), pair_tile("w2_b")
         deal(w2_a[:], w2_raw, 0, nc.scalar.copy)
-        deal(w2_b[:], w2_raw, 1, nc.vector.tensor_copy)
-        w2_q = quantize_weight("w2_qa", w2_a[:]) + quantize_weight("w2_qb", w2_b[:])
+        deal(w2_b[:], w2_raw, 1, nc.scalar.copy)
+        w2_q = quantize_weight("w2_qa", w2_a[:])
         x1_scales = pick("x1_scales", table_scales[:], offs_sb, U8, tag="w2_a")
+        w2_q = w2_q + quantize_weight("w2_qb", w2_b[:])
 
         gain_abs = sb.tile([P, PACK], F32, name="gain_abs")
         nc.scalar.activation(gain_abs[:], gain[:], ACT.Abs)
@@ -174,23 +175,28 @@ def tile_picked_twlclampbminmod_none_p_kernel(
         deal(w3_b[:], w3_raw, 1, nc.scalar.copy)
 
         last = PACK - 1
-        z = [sb.tile([P, HALF, PACK], BF16, name="z%d" % c, align_bytes=64) for c in range(2)]
+        pieces = [slice(0, 256), slice(256, 384), slice(384, 512)]
+        z = [
+            sb.tile([P, cols.stop - cols.start, PACK], BF16, name="z%d" % i, align_bytes=64)
+            for i, cols in enumerate(pieces)
+        ]
+        d3_pieces = [d3[0], d3[1][:, :, 0:128], d3[1][:, :, 128:256]]
         z_codes = sb.tile([P, S], U32, name="z_codes", align_bytes=64)
         z_scales = sb.tile([P, S], U8, name="z_scales", align_bytes=64)
 
         def smaller(tiles):
             nc.vector.tensor_tensor(d2[:, tiles, :], d2[:, tiles, :], a_round[:, tiles, :], ALU.min)
 
-        def larger(c):
+        def larger(i):
             runs = "p t (g i) -> p g t i"
             nc.vector.tensor_tensor(
-                z[c][:].rearrange("p (g i) t -> p g t i", i=RUN),
-                d2[:, :, half(c)].rearrange(runs, i=RUN), d3[c].rearrange(runs, i=RUN), ALU.max,
+                z[i][:].rearrange("p (g i) t -> p g t i", i=RUN),
+                d2[:, :, pieces[i]].rearrange(runs, i=RUN), d3_pieces[i].rearrange(runs, i=RUN), ALU.max,
             )
 
-        def quantize_z(c):
+        def quantize_z(i):
             nc.vector.quantize_mx(
-                z_codes[:, half(c)].bitcast(FP8X4), z_scales[:, half(c)], z[c][:].rearrange("p s t -> p (s t)")
+                z_codes[:, pieces[i]].bitcast(FP8X4), z_scales[:, pieces[i]], z[i][:].rearrange("p s t -> p (s t)")
             )
 
         smaller(slice(0, last))
@@ -203,21 +209,35 @@ def tile_picked_twlclampbminmod_none_p_kernel(
         quantize_z(0)
         gather_d3(1, 3)
         larger(1)
-        w3_q = w3_q + quantize_weight("w3_q1", w3_a[:, 1:2], tag="d_n2")
+        larger(2)
         quantize_z(1)
-        w3_q = w3_q + quantize_weight("w3_qb", w3_b[:], tag="z1")
+        quantize_z(2)
+        w3_q = w3_q + quantize_weight("w3_q1", w3_a[:, 1:2], tag="z1")
+        w3_q = w3_q + quantize_weight("w3_qb", w3_b[:], tag="z2")
 
         h, h_neg = wide_a, wide_b
 
-        def second_layer(t, cols, bank):
+        def multiply(t, cols, bank):
             product(bank[:, cols], w3_q[t], z_codes[:, cols], z_scales[:, cols])
-            nc.scalar.activation(h_neg[t][:, cols], bank[:, cols], ACT.Copy, scale=-1.0)
+
+        def copy_h(t, cols, bank):
             nc.scalar.copy(h[t][:, cols], bank[:, cols])
 
-        second_layer(0, half(0), banks[PACK])
-        second_layer(0, half(1), banks[0])
+        def copy_h_neg(t, cols, bank):
+            nc.scalar.activation(h_neg[t][:, cols], bank[:, cols], ACT.Copy, scale=-1.0)
+
+        piece_banks = [banks[PACK], banks[PACK + 1], banks[0]]
+        for cols, bank in zip(pieces, piece_banks):
+            multiply(0, cols, bank)
+            copy_h(0, cols, bank)
+            if cols is pieces[0]:
+                copy_h_neg(0, cols, bank)
+        for cols, bank in zip(pieces[1:], piece_banks[1:]):
+            copy_h_neg(0, cols, bank)
         for t in range(1, PACK):
-            second_layer(t, every, banks[t])
+            multiply(t, every, banks[t])
+            copy_h(t, every, banks[t])
+            copy_h_neg(t, every, banks[t])
 
         pa = [sb.tile([P, S], F32, name="pa%d" % t) for t in range(PACK)]
         pb = [sb.tile([P, S], F32, name="pb%d" % t) for t in range(PACK)]
@@ -233,24 +253,27 @@ def tile_picked_twlclampbminmod_none_p_kernel(
         def lower(t, cols):
             nc.vector.scalar_tensor_tensor(pa[t][:, cols], pb[t][:, cols], 0.0, pa[t][:, cols], ALU.min, ALU.max)
 
-        def upper(t, cols):
+        def upper(t, cols, queue):
             nc.vector.scalar_tensor_tensor(res[t][:, cols], pb[t][:, cols], 0.0, pa[t][:, cols], ALU.max, ALU.min)
-            nc.sync.dma_start(out_rows[t][:, cols], res[t][:, cols])
+            queue.dma_start(out_rows[t][:, cols], res[t][:, cols])
 
-        for t in range(last):
-            gather_pa(t, every)
-            if t > 0:
-                lower(t - 1, every)
+        gather_pb(0, half(0))
+        gather_pb(0, half(1))
+        gather_pa(0, every)
+        for t in range(1, last):
             gather_pb(t, every)
-            if t > 0:
-                upper(t - 1, every)
-        gather_pa(last, half(0))
-        lower(last - 1, every)
+            lower(t - 1, every)
+            gather_pa(t, every)
+            upper(t - 1, every, nc.sync)
         gather_pb(last, half(0))
-        upper(last - 1, every)
-        gather_pa(last, half(1))
-        lower(last, half(0))
+        lower(last - 1, every)
+        gather_pa(last, half(0))
+        upper(last - 1, every, nc.sync)
         gather_pb(last, half(1))
-        upper(last, half(0))
-        lower(last, half(1))
-        upper(last, half(1))
+        lower(last, half(0))
+        gather_pa(last, half(1))
+        upper(last, half(0), nc.sync)
+        lower(last, pieces[1])
+        lower(last, pieces[2])
+        upper(last, pieces[1], nc.scalar)
+        upper(last, pieces[2], nc.sync)

from contextlib import ExitStack

import concourse.mybir as mybir

K, T, S, N, H = 512, 2048, 512, 512, 512
FLOPS = 2 * S * (2 * K * H + H * N)

F32 = mybir.dt.float32
BF16 = mybir.dt.bfloat16
I32 = mybir.dt.int32
U32 = mybir.dt.uint32
U16 = mybir.dt.uint16
U8 = mybir.dt.uint8
FP8X4 = mybir.dt.float8_e4m3fn_x4
ALU = mybir.AluOpType
ACT = mybir.ActivationFunctionType

P = 128
PACK = 4
HALF = S // 2
RUN = 8


def tile_picked_twlclampbminmod_none_p_kernel(
    tc, x_words, x_scales, w1, w2, gn, w3, offs, two, n1, n2, n3, n4, n5, out
):
    nc = tc.nc
    with ExitStack() as ctx:
        lists = ctx.enter_context(tc.tile_pool(name="lists", bufs=1))
        sb = ctx.enter_context(tc.tile_pool(name="sb", bufs=1))
        psum = ctx.enter_context(tc.psum_pool(name="psum", bufs=1))

        def load_list(name, src):
            dst = lists.tile([P, S // 16], U16, name=name)
            nc.sync.dma_start(dst[:], src)
            return dst

        def load_weight(name, src):
            dst = sb.tile([P, PACK, 512], F32, name=name)
            nc.sync.dma_start(dst[:], src.rearrange("(p j) c -> p j c", j=PACK))
            return dst

        table_scales = sb.tile([P, T], U8, name="table_scales", align_bytes=64)
        nc.vector.memset(table_scales[:].bitcast(I32), 0)

        table_words = sb.tile([P, T], I32, name="table_words", align_bytes=64)
        nc.sync.dma_start(table_words[:], x_words[0].rearrange("p n r -> p (n r)").bitcast(I32))
        two_sb = load_list("two_sb", two)
        offs_sb = load_list("offs_sb", offs)
        for q in range(4):
            nc.sync.dma_start(
                table_scales[32 * q : 32 * q + 4, :].bitcast(I32), x_scales[0, 4 * q : 4 * q + 4, :].bitcast(I32)
            )
        w2_raw = load_weight("w2_raw", w2)
        gain = sb.tile([P, PACK], F32, name="gain")
        nc.sync.dma_start(gain[:], gn.rearrange("(p t) o -> p (t o)", t=PACK))
        n2_sb = load_list("n2_sb", n2)
        w1_raw = load_weight("w1_raw", w1)
        n3_sb = load_list("n3_sb", n3)
        n1_sb = load_list("n1_sb", n1)
        w3_raw = load_weight("w3_raw", w3)
        n4_sb = load_list("n4_sb", n4)
        n5_sb = load_list("n5_sb", n5)

        wide_a = [sb.tile([P, 2 * S], F32, name="wide_a%d" % t) for t in range(PACK)]
        wide_b = [sb.tile([P, 2 * S], F32, name="wide_b%d" % t) for t in range(PACK)]
        d = [sb.tile([P, 2 * S], F32, name="d%d" % t) for t in range(PACK)]
        for wide in d + wide_a[:1]:
            nc.vector.memset(wide[:, S:], 0.0)

        def pick(name, window, offsets, dtype, tag=""):
            dst = sb.tile([P, S], dtype, name=name, tag=tag, align_bytes=64)
            nc.vector.tensor_copy(dst[:], window.indirect(offsets[:]))
            return dst

        def deal(dealt, raw, pair, copy):
            copy(
                dealt.rearrange("p t m j -> p m j t"),
                raw[:].rearrange("p j (m t) -> p m j t", t=PACK)[:, :, :, 2 * pair : 2 * pair + 2],
            )

        def pair_tile(name):
            return sb.tile([P, 2, P, PACK], BF16, name=name, align_bytes=64)

        def quantize(name, values, width, tag=""):
            codes = sb.tile([P, width], U32, name=name + "_codes", tag=tag, align_bytes=64)
            scales = sb.tile([P, width], U8, name=name + "_scales", align_bytes=64)
            nc.vector.quantize_mx(codes[:].bitcast(FP8X4), scales[:], values)
            return codes, scales

        def quantize_weight(name, dealt, tag=""):
            return column_tiles(quantize(name, dealt.rearrange("p t m j -> p (t m j)"), dealt.shape[1] * P, tag))

        def product(dst, weight, codes, scales):
            nc.tensor.matmul_mx(
                dst, lhsT=weight[0].bitcast(FP8X4), lhsT_scale=weight[1],
                rhs=codes.bitcast(FP8X4), rhs_scale=scales, start=True, stop=True,
            )

        def column_tiles(quantized):
            codes, scales = quantized
            return [(codes[:, c : c + P], scales[:, c : c + P]) for c in range(0, codes.shape[1], P)]

        def half(c):
            return slice(c * HALF, (c + 1) * HALF)

        def look(window, offsets, cols):
            return window[:].indirect(offsets[:, cols.start // 16 : cols.stop // 16])

        banks = [psum.tile([P, S], F32, name="bank%d" % b) for b in range(8)]

        x2_words = pick("x2_words", table_words[:].bitcast(U32), two_sb, U32)
        x1_words = pick("x1_words", table_words[:].bitcast(U32), offs_sb, U32)
        x2_scales = pick("x2_scales", table_scales[:], two_sb, U8)
        w2_a, w2_b = pair_tile("w2_a"), pair_tile("w2_b")
        deal(w2_a[:], w2_raw, 0, nc.scalar.copy)
        deal(w2_b[:], w2_raw, 1, nc.scalar.copy)
        w2_q = quantize_weight("w2_qa", w2_a[:])
        x1_scales = pick("x1_scales", table_scales[:], offs_sb, U8, tag="w2_a")
        w2_q = w2_q + quantize_weight("w2_qb", w2_b[:])

        gain_abs = sb.tile([P, PACK], F32, name="gain_abs")
        nc.scalar.activation(gain_abs[:], gain[:], ACT.Abs)
        gain_half = sb.tile([P, PACK], F32, name="gain_half")
        nc.scalar.activation(gain_half[:], gain_abs[:], ACT.Copy, scale=-0.5)
        gain_ge = sb.tile([P, PACK], F32, name="gain_ge")
        nc.gpsimd.tensor_scalar(gain_ge[:], gain[:], 0.0, 2.0, ALU.is_ge, ALU.mult)
        gain_sign = sb.tile([P, PACK], F32, name="gain_sign")
        nc.gpsimd.tensor_scalar(gain_sign[:], gain_ge[:], 1.0, -1.0, ALU.mult, ALU.add)

        for t in range(PACK):
            product(banks[PACK + t][:], w2_q[t], x2_words[:], x2_scales[:])
            nc.scalar.activation(d[t][:, 0:S], banks[PACK + t][:], ACT.Copy, scale=gain_abs[:, t : t + 1])

        w1_dealt = sb.tile([P, PACK, P, PACK], BF16, name="w1_dealt", tag="w1_then_d3", align_bytes=64)
        for pair in range(2):
            deal(w1_dealt[:, 2 * pair : 2 * pair + 2], w1_raw, pair, nc.scalar.copy)

        every = slice(0, S)
        d2 = sb.tile([P, PACK, S], BF16, name="d_n2", align_bytes=64)
        for t in range(PACK):
            nc.vector.tensor_copy(d2[:, t, :], look(d[t], n2_sb, every))
        w1_q = quantize_weight("w1_qa", w1_dealt[:, 0:2]) + quantize_weight("w1_qb", w1_dealt[:, 2:4])

        def gather_d3(c, t):
            nc.vector.tensor_copy(d3[c][:, t, :], look(d[t], n3_sb, half(c)))

        def sign_w3(j):
            nc.scalar.activation(w3_raw[:, j, :], w3_raw[:, j, :], ACT.Copy, scale=gain_sign[:, j : j + 1])

        a_round = sb.tile([P, PACK, S], BF16, name="a_round")
        d3_first = sb.tile([P, PACK, HALF], BF16, name="d3_first", tag="w1_then_d3", align_bytes=64)
        d3 = [d3_first[:], a_round[:, :, half(0)]]
        for t in range(PACK):
            gather_d3(0, t)
        sign_w3(0)
        sign_w3(1)

        y_half = wide_a
        y_last = sb.tile([P, S], F32, name="y3", align_bytes=64)
        y = [wide_a[t + 1][:, S:] for t in range(PACK - 1)] + [y_last[:]]
        a = [wide_b[t][:, S:] for t in range(PACK)]
        for t in range(PACK):
            product(banks[t][:], w1_q[t], x1_words[:], x1_scales[:])
            nc.scalar.activation(y_half[t][:, every], banks[t][:], ACT.Copy, scale=gain_half[:, t : t + 1])
            nc.scalar.activation(y[t], banks[t][:], ACT.Copy, scale=gain_abs[:, t : t + 1])
            nc.vector.tensor_tensor(a[t], look(y_half[t], n1_sb, every), y[t], ALU.add)
        for t in range(PACK):
            nc.scalar.copy(a_round[:, t, :], a[t])

        sign_w3(2)
        sign_w3(3)
        w3_a, w3_b = pair_tile("w3_a"), pair_tile("w3_b")
        deal(w3_a[:], w3_raw, 0, nc.scalar.copy)
        deal(w3_b[:], w3_raw, 1, nc.scalar.copy)

        last = PACK - 1
        pieces = [slice(0, 256), slice(256, 384), slice(384, 512)]
        z = [
            sb.tile([P, cols.stop - cols.start, PACK], BF16, name="z%d" % i, align_bytes=64)
            for i, cols in enumerate(pieces)
        ]
        d3_pieces = [d3[0], d3[1][:, :, 0:128], d3[1][:, :, 128:256]]
        z_codes = sb.tile([P, S], U32, name="z_codes", align_bytes=64)
        z_scales = sb.tile([P, S], U8, name="z_scales", align_bytes=64)

        def smaller(tiles):
            nc.vector.tensor_tensor(d2[:, tiles, :], d2[:, tiles, :], a_round[:, tiles, :], ALU.min)

        def larger(i):
            runs = "p t (g i) -> p g t i"
            nc.vector.tensor_tensor(
                z[i][:].rearrange("p (g i) t -> p g t i", i=RUN),
                d2[:, :, pieces[i]].rearrange(runs, i=RUN), d3_pieces[i].rearrange(runs, i=RUN), ALU.max,
            )

        def quantize_z(i):
            nc.vector.quantize_mx(
                z_codes[:, pieces[i]].bitcast(FP8X4), z_scales[:, pieces[i]], z[i][:].rearrange("p s t -> p (s t)")
            )

        smaller(slice(0, last))
        gather_d3(1, 0)
        smaller(slice(last, PACK))
        gather_d3(1, 1)
        larger(0)
        w3_q = quantize_weight("w3_q0", w3_a[:, 0:1])
        gather_d3(1, 2)
        quantize_z(0)
        gather_d3(1, 3)
        larger(1)
        larger(2)
        quantize_z(1)
        quantize_z(2)
        w3_q = w3_q + quantize_weight("w3_q1", w3_a[:, 1:2], tag="z1")
        w3_q = w3_q + quantize_weight("w3_qb", w3_b[:], tag="z2")

        h, h_neg = wide_a, wide_b

        def multiply(t, cols, bank):
            product(bank[:, cols], w3_q[t], z_codes[:, cols], z_scales[:, cols])

        def copy_h(t, cols, bank):
            nc.scalar.copy(h[t][:, cols], bank[:, cols])

        def copy_h_neg(t, cols, bank):
            nc.scalar.activation(h_neg[t][:, cols], bank[:, cols], ACT.Copy, scale=-1.0)

        piece_banks = [banks[PACK], banks[PACK + 1], banks[0]]
        for cols, bank in zip(pieces, piece_banks):
            multiply(0, cols, bank)
            copy_h(0, cols, bank)
            if cols is pieces[0]:
                copy_h_neg(0, cols, bank)
        for cols, bank in zip(pieces[1:], piece_banks[1:]):
            copy_h_neg(0, cols, bank)
        for t in range(1, PACK):
            multiply(t, every, banks[t])
            copy_h(t, every, banks[t])
            copy_h_neg(t, every, banks[t])

        pa = [sb.tile([P, S], F32, name="pa%d" % t) for t in range(PACK)]
        pb = [sb.tile([P, S], F32, name="pb%d" % t) for t in range(PACK)]
        res = [sb.tile([P, S], F32, name="res%d" % t) for t in range(PACK)]
        out_rows = out.rearrange("(p t) s -> t p s", t=PACK)

        def gather_pa(t, cols):
            nc.vector.tensor_tensor(pa[t][:, cols], look(h_neg[t], n4_sb, cols), h[t][:, cols], ALU.add)

        def gather_pb(t, cols):
            nc.vector.tensor_tensor(pb[t][:, cols], look(h[t], n5_sb, cols), h_neg[t][:, cols], ALU.add)

        def lower(t, cols):
            nc.vector.scalar_tensor_tensor(pa[t][:, cols], pb[t][:, cols], 0.0, pa[t][:, cols], ALU.min, ALU.max)

        def upper(t, cols, queue):
            nc.vector.scalar_tensor_tensor(res[t][:, cols], pb[t][:, cols], 0.0, pa[t][:, cols], ALU.max, ALU.min)
            queue.dma_start(out_rows[t][:, cols], res[t][:, cols])

        gather_pb(0, half(0))
        gather_pb(0, half(1))
        gather_pa(0, every)
        for t in range(1, last):
            gather_pb(t, every)
            lower(t - 1, every)
            gather_pa(t, every)
            upper(t - 1, every, nc.sync)
        gather_pb(last, half(0))
        lower(last - 1, every)
        gather_pa(last, half(0))
        upper(last - 1, every, nc.sync)
        gather_pb(last, half(1))
        lower(last, half(0))
        gather_pa(last, half(1))
        upper(last, half(0), nc.sync)
        lower(last, pieces[1])
        lower(last, pieces[2])
        upper(last, pieces[1], nc.scalar)
        upper(last, pieces[2], nc.sync)
